import numpy as np
import ml_dtypes


def mxq(x, axis, fmt="e4m3"):
    dtype, down = {"e4m3": (ml_dtypes.float8_e4m3fn, 7), "e5m2": (ml_dtypes.float8_e5m2, 14)}[fmt]
    v = np.moveaxis(np.asarray(x, np.float32).astype(ml_dtypes.bfloat16).astype(np.float64), axis, -1)
    blocks = v.reshape(v.shape[:-1] + (-1, 32))
    amax = np.abs(blocks).max(-1, keepdims=True)
    byte = np.maximum(np.where(amax > 0, np.frexp(amax)[1] - 1 + 127, 0) - down, 1)
    scale = np.exp2(byte - 127.0)
    codes = (blocks / scale).astype(np.float32).astype(dtype).astype(np.float64)
    return np.moveaxis((codes * scale).reshape(v.shape), -1, axis)


WIDE = False


def mx_kscale(k):
    if not WIDE:
        return np.ones(k)
    levels = np.array([30, -30])
    if k % 512:
        return np.exp2(np.random.permutation(np.resize(levels, k // 32))).repeat(32)
    a = np.empty((k // 512, 16))
    for p in range(k // 512):
        a[p, :8] = np.random.permutation(np.resize(levels, 8))
        for g in range(8):
            far = levels[np.abs(levels - a[p, g]) >= 10]
            a[p, g + 8] = far[np.random.randint(len(far))]
    return np.exp2(a.ravel()).repeat(32)


def f64(x):
    return np.asarray(x).astype(np.float64)


def striped(idx):
    return np.tile(np.asarray(idx).reshape(-1, 16).T, (8, 1)).astype(np.uint16)


def unstriped(offs):
    return offs[:16].T.reshape(-1).astype(np.int64)


def striped8(idx):
    return np.asarray(idx).reshape(8, -1, 16).transpose(0, 2, 1).reshape(128, -1).astype(np.uint16)


def unstriped8(offs):
    return offs.reshape(8, 16, -1).transpose(0, 2, 1).reshape(8, -1).astype(np.int64)


def pick8(x, idx, run):
    r = np.arange(len(x))
    return x[r[:, None], idx[r % (8 * run) // run]]


E2M1 = np.array([0.0, 0.5, 1.0, 1.5, 2.0, 3.0, 4.0, 6.0, -0.0, -0.5, -1.0, -1.5, -2.0, -3.0, -4.0, -6.0])


def pack_weight(w, fmt):
    k, n = w.shape
    w = f64(np.asarray(w, np.float32).astype(ml_dtypes.bfloat16)).reshape(k // 32, 32, n)
    amax = np.abs(w).max(1)
    if fmt in ("e4m3", "e5m2"):
        byte = np.frexp(amax)[1] - 1 + 127 - (7 if fmt == "e4m3" else 14)
    else:
        mant, ex = np.frexp(amax / 6.0)
        byte = np.where(mant > 0.5, ex, ex - 1) + 127
    byte = np.clip(np.where(amax > 0, byte, 1), 1, 254)
    scaled = (w * np.exp2(127.0 - byte)[:, None, :]).reshape(k, n).astype(np.float32)
    by_word = np.ascontiguousarray(scaled.reshape(k // 512, 128, 4, n).transpose(0, 1, 3, 2))
    if fmt in ("e4m3", "e5m2"):
        words = by_word.astype(ml_dtypes.float8_e4m3fn if fmt == "e4m3" else ml_dtypes.float8_e5m2).view(np.uint8)
    else:
        c = by_word.astype(ml_dtypes.float4_e2m1fn).view(np.uint8) & 0xF
        words = (c[..., 0::2] | (c[..., 1::2] << 4)).reshape(k // 512, 128, 2 * n)
    return np.ascontiguousarray(words), np.ascontiguousarray(byte.astype(np.uint8).reshape(k // 512, 16, n))


def unpack_weight(words, scales, fmt):
    g, _, n = scales.shape
    words = np.ascontiguousarray(words).reshape(g, 128, n, -1)
    if fmt in ("e4m3", "e5m2"):
        vals = words.view(ml_dtypes.float8_e4m3fn if fmt == "e4m3" else ml_dtypes.float8_e5m2).astype(np.float64)
    else:
        nib = np.empty((g, 128, n, 4), np.uint8)
        nib[..., 0::2] = words & 0xF
        nib[..., 1::2] = words >> 4
        vals = E2M1[nib]
    vals = vals * np.repeat(np.exp2(scales.astype(np.float64) - 127.0), 8, axis=1)[..., None]
    return vals.transpose(0, 1, 3, 2).reshape(g * 512, n)


def sigmoid(v):
    return 1.0 / (1.0 + np.exp(-v))


def sgn(shape):
    return np.random.uniform(0.5, 2.0, shape) * np.where(np.random.standard_normal(shape) < 0, -1.0, 1.0)


K, T, J, R, C, O, N, S, U, E = 512, 1024, 256, 512, 512, 256, 256, 1024, 128, 512


def setup_inputs():
    n = np.random.standard_normal
    idx = np.random.permutation(T)[:J]
    idx2 = np.stack([np.random.permutation(C)[:J] for _ in range(8)])
    idx3 = np.stack([np.random.permutation(C)[:O] for _ in range(8)])
    idx4 = np.stack([np.random.permutation(C)[:O] for _ in range(8)])
    idx5 = np.random.permutation(S)[:N]
    idx6 = np.random.permutation(O)[:U]
    idx7 = np.random.permutation(E)[:U]
    fk = mx_kscale(K)
    fr = mx_kscale(R)
    xtp = pack_weight(n((K, T)) / fk[:, None], "e5m2")
    wp = pack_weight(n((K, R)) * 1 / np.sqrt(K) * fk[:, None], "e2m1")
    vsp = pack_weight(n((R, S)) * 1 / np.sqrt(R) / fr[:, None], "e2m1")
    return {
        "xt_words": xtp[0],
        "xt_scales": xtp[1],
        "w_words": wp[0],
        "w_scales": wp[1],
        "sa": (np.random.uniform(0.5, 1.6, (R, 1)) * fr[:, None]).astype(np.float32),
        "sg": (sgn((R, 1))).astype(np.float32),
        "bg": (np.random.uniform(-2.0, 2.0, (R, 1))).astype(np.float32),
        "vs_words": vsp[0],
        "vs_scales": vsp[1],
        "so": (sgn((N, 1))).astype(np.float32),
        "offs": striped(idx),
        "offs2": striped8(idx2),
        "offs3": striped8(idx3),
        "offs4": striped8(idx4),
        "offs5": striped(idx5),
        "offs6": striped(idx6),
        "offs7": striped(idx7),
    }


def reference(xt_words, xt_scales, w_words, w_scales, sa, sg, bg, vs_words, vs_scales, so, offs, offs2, offs3, offs4, offs5, offs6, offs7):
    idx = unstriped(offs)
    idx2 = unstriped8(offs2)
    idx3 = unstriped8(offs3)
    idx4 = unstriped8(offs4)
    idx5 = unstriped(offs5)
    idx6 = unstriped(offs6)
    idx7 = unstriped(offs7)
    xtu = unpack_weight(xt_words, xt_scales, "e5m2")
    wu = unpack_weight(w_words, w_scales, "e2m1")
    vsu = unpack_weight(vs_words, vs_scales, "e2m1")
    xtidxg = xtu[:, idx]
    a = wu.T @ xtidxg
    pw = np.zeros((R, C))
    pw[np.arange(R)[:, None], idx2[np.arange(R) % 512 // 64]] = a
    hid = pick8(pw, idx3, 64) * f64(sa) * sigmoid(pick8(pw, idx4, 64) * f64(sg) + f64(bg))
    vsidx5g = vsu[:, idx5]
    hidq = mxq(hid, 0, "e4m3")
    p = vsidx5g.T @ hidq
    m0 = p[:, idx6] * f64(so)
    y = np.zeros((N, E))
    y[:, idx7] = m0
    return y

@@ -1,0 +1,189 @@
+from contextlib import ExitStack
+
+import concourse.mybir as mybir
+
+K, T, J, R, C, O, N, S, U, E = 512, 1024, 256, 512, 512, 256, 256, 1024, 128, 512
+FLOPS = 2 * K * R * J + 2 * R * N * O
+
+F32 = mybir.dt.float32
+BF16 = mybir.dt.bfloat16
+I32 = mybir.dt.int32
+U32 = mybir.dt.uint32
+U16 = mybir.dt.uint16
+U8 = mybir.dt.uint8
+E4M3X4 = mybir.dt.float8_e4m3fn_x4
+E5M2X4 = mybir.dt.float8_e5m2_x4
+E2M1X4 = mybir.dt.float4_e2m1fn_x4
+ACT = mybir.ActivationFunctionType
+MULT = mybir.AluOpType.mult
+
+P = 128
+PACK = 4
+HALF = 128
+
+
+def tile_list_gatedgroupboard_solo_store_postedout_kernel(
+    tc, xt_words, xt_scales, w_words, w_scales, sa, sg, bg, vs_words, vs_scales, so,
+    offs, offs2, offs3, offs4, offs5, offs6, offs7, out,
+):
+    nc = tc.nc
+    with ExitStack() as ctx:
+        lists = ctx.enter_context(tc.tile_pool(name="lists", bufs=1))
+        sb = ctx.enter_context(tc.tile_pool(name="sb", bufs=1))
+        psum = ctx.enter_context(tc.psum_pool(name="psum", bufs=1))
+
+        def list_tile(src, name):
+            return lists.tile([P, src.shape[1]], U16, name=name)
+
+        l1, l2, l3, l4, l5, l6, l7 = [
+            list_tile(src, "list%d" % i) for i, src in enumerate((offs, offs2, offs3, offs4, offs5, offs6, offs7))
+        ]
+
+        def half(lst, h):
+            return lst[:, h * (HALF // 16) : (h + 1) * (HALF // 16)]
+
+        xs_stage = sb.tile([4, 4, T // 4], I32, name="xs_stage")
+        ws_stage = sb.tile([4, 4, R // 4], I32, name="ws_stage")
+        xw_win = sb.tile([P, T], U32, name="xw_win")
+        xs_win = sb.tile([P, T], U8, name="xs_win")
+        ww_raw = sb.tile([P, R], U16, name="ww_raw")
+        ws_raw = sb.tile([P, R], U8, name="ws_raw")
+        vw_win = sb.tile([P, S], U16, name="vw_win")
+        vs_win = sb.tile([P, S], U8, name="vs_win")
+        sa_sb = sb.tile([P, PACK], F32, name="sa_sb")
+        sg_sb = sb.tile([P, PACK], F32, name="sg_sb")
+        bg_sb = sb.tile([P, PACK], F32, name="bg_sb")
+        so_sb = [sb.tile([P, 1], F32, name="so_sb%d" % m) for m in range(2)]
+        boards = [sb.tile([P, C], F32, name="board%d" % t) for t in range(PACK)]
+        pages = [sb.tile([P, E], F32, name="page%d" % m) for m in range(2)]
+
+        nc.vector.memset(xs_win[:].bitcast(I32), 0)
+        nc.vector.memset(ws_raw[:].bitcast(I32), 0)
+        nc.vector.memset(vs_win[:].bitcast(I32), 0)
+        for board in boards:
+            nc.vector.memset(board[:], 0.0)
+        for page in pages:
+            nc.vector.memset(page[:], 0.0)
+
+        def staged(scales):
+            return scales[0].rearrange("(q r) c -> r q c", r=4).bitcast(I32)
+
+        nc.sync.dma_start(xs_stage[:], staged(xt_scales))
+        nc.scalar.dma_start(ws_stage[:], staged(w_scales))
+        nc.sync.dma_start(l1[:], offs)
+        nc.sync.dma_start(xw_win[:].bitcast(I32), xt_words[0].rearrange("p n t -> p (n t)").bitcast(I32))
+        nc.sync.dma_start(ww_raw[:].bitcast(I32), w_words[0].bitcast(I32))
+        nc.sync.dma_start(l2[:], offs2)
+        nc.sync.dma_start(l4[:], offs4)
+        nc.sync.dma_start(l3[:], offs3)
+        nc.gpsimd.dma_start(sg_sb[:], sg.rearrange("(p t) o -> p (t o)", t=PACK))
+        nc.gpsimd.dma_start(bg_sb[:], bg.rearrange("(p t) o -> p (t o)", t=PACK))
+        nc.gpsimd.dma_start(sa_sb[:], sa.rearrange("(p t) o -> p (t o)", t=PACK))
+        for m in range(2):
+            nc.gpsimd.dma_start(so_sb[m][:], so[m * P : (m + 1) * P, :])
+        nc.sync.dma_start(vw_win[:].bitcast(I32), vs_words[0].bitcast(I32))
+        nc.sync.dma_start(l5[:], offs5)
+        for q in range(4):
+            nc.sync.dma_start(vs_win[32 * q : 32 * q + 4, :].bitcast(I32), vs_scales[0, 4 * q : 4 * q + 4, :].bitcast(I32))
+        nc.sync.dma_start(l6[:], offs6)
+        nc.sync.dma_start(l7[:], offs7)
+
+        xw = sb.tile([P, J], U32, name="xw", align_bytes=64)
+        xs = sb.tile([P, J], U8, name="xs", align_bytes=128)
+        ww = sb.tile([P, PACK, P], U16, name="ww", align_bytes=64)
+        ws = sb.tile([P, PACK, P], U8, name="ws", align_bytes=64)
+
+        def cols(h):
+            return slice(h * HALF, (h + 1) * HALF)
+
+        for q in range(4):
+            nc.vector.tensor_copy(xs_win[32 * q : 32 * q + 4, :].bitcast(I32), xs_stage[:, q, :])
+        nc.vector.tensor_copy(xs[:, cols(0)], xs_win[:].indirect(half(l1, 0)))
+        for q in range(4):
+            nc.vector.tensor_copy(ws_raw[32 * q : 32 * q + 4, :].bitcast(I32), ws_stage[:, q, :])
+        ws_dealt = ws_raw[:].rearrange("p (m t) -> p t m", t=PACK)
+        ww_dealt = ww_raw[:].rearrange("p (m t) -> p t m", t=PACK)
+        nc.vector.tensor_copy(ws[:], ws_dealt)
+        for t in range(PACK):
+            nc.scalar.copy(ww[:, t, :], ww_dealt[:, t, :])
+        nc.vector.tensor_copy(xw[:, cols(0)], xw_win[:].indirect(half(l1, 0)))
+        nc.vector.tensor_copy(xw[:, cols(1)], xw_win[:].indirect(half(l1, 1)))
+        nc.vector.tensor_copy(xs[:, cols(1)], xs_win[:].indirect(half(l1, 1)))
+
+        a_sb = [sb.tile([P, J], F32, name="a_sb%d" % t) for t in range(PACK)]
+
+        def first_product(t, js, bank):
+            acc = psum.tile([P, js.stop - js.start], F32, name="acc", tag="bank%d" % bank)
+            nc.tensor.matmul_mx(
+                out=acc[:], lhsT=ww[:, t, :].bitcast(E2M1X4), lhsT_scale=ws[:, t, :],
+                rhs=xw[:, js].bitcast(E5M2X4), rhs_scale=xs[:, js], start=True, stop=True,
+            )
+            nc.scalar.copy(a_sb[t][:, js], acc[:])
+
+        first_product(0, cols(0), 0)
+        first_product(0, cols(1), 1)
+        for t in range(1, PACK):
+            first_product(t, slice(0, J), 1 + t)
+
+        value = sb.tile([P, PACK, O], F32, name="value")
+        gate = sb.tile([P, PACK, O], F32, name="gate")
+
+        def look(t, places, offs_value, offs_gate):
+            nc.scalar.activation(
+                out=gate[:, t, places], in_=boards[t][:].indirect(offs_gate), func=ACT.Sigmoid,
+                bias=bg_sb[:, t : t + 1], scale=sg_sb[:, t : t + 1],
+            )
+            nc.scalar.activation(
+                out=value[:, t, places], in_=boards[t][:].indirect(offs_value), func=ACT.Copy, scale=sa_sb[:, t : t + 1],
+            )
+
+        for t in range(PACK):
+            if t == 0:
+                for h in range(2):
+                    nc.vector.tensor_copy(boards[t][:].indirect(half(l2, h)), a_sb[t][:, cols(h)])
+            else:
+                nc.vector.tensor_copy(boards[t][:].indirect(l2[:]), a_sb[t][:])
+            if t == PACK - 1:
+                for h in range(2):
+                    look(t, cols(h), half(l3, h), half(l4, h))
+            else:
+                look(t, slice(0, O), l3[:], l4[:])
+
+        vw = sb.tile([P, N], U16, name="vw", align_bytes=64)
+        vsc = sb.tile([P, N], U8, name="vsc", align_bytes=128)
+        nc.vector.tensor_copy(vw[:], vw_win[:].indirect(l5[:]))
+        nc.vector.tensor_copy(vsc[:], vs_win[:].indirect(l5[:]))
+
+        hid = [sb.tile([P, HALF, PACK], BF16, name="hid%d" % h, align_bytes=64) for h in range(2)]
+        hw = [sb.tile([P, HALF], U32, name="hw%d" % h, align_bytes=64) for h in range(2)]
+        hs = [sb.tile([P, HALF], U8, name="hs%d" % h, align_bytes=64) for h in range(2)]
+        for h in range(2):
+            nc.vector.tensor_tensor(
+                hid[h][:].rearrange("p (c i) t -> p c t i", i=4),
+                value[:, :, cols(h)].rearrange("p t (c i) -> p c t i", i=4),
+                gate[:, :, cols(h)].rearrange("p t (c i) -> p c t i", i=4),
+                MULT,
+            )
+        for h in range(2):
+            nc.vector.quantize_mx(out=hw[h][:].bitcast(E4M3X4), scales=hs[h][:], in_=hid[h][:].rearrange("p o t -> p (o t)"))
+
+        p_sb = [sb.tile([P, O], F32, name="p_sb%d" % m) for m in range(2)]
+        for h in range(2):
+            for m in range(2):
+                acc = psum.tile([P, HALF], F32, name="acc2", tag="bank%d" % ((5 + 2 * h + m) % 8))
+                nc.tensor.matmul_mx(
+                    out=acc[:], lhsT=vw[:, cols(m)].bitcast(E2M1X4), lhsT_scale=vsc[:, cols(m)],
+                    rhs=hw[h][:].bitcast(E4M3X4), rhs_scale=hs[h][:], start=True, stop=True,
+                )
+                if m == 0:
+                    nc.scalar.copy(p_sb[m][:, cols(h)], acc[:])
+                else:
+                    nc.vector.tensor_copy(p_sb[m][:, cols(h)], acc[:])
+
+        ends = [sb.tile([P, U], F32, name="ends%d" % m) for m in range(2)]
+        for m in range(2):
+            nc.scalar.activation(out=ends[m][:], in_=p_sb[m][:].indirect(l6[:]), func=ACT.Copy, scale=so_sb[m][:])
+        nc.vector.tensor_copy(pages[0][:].indirect(l7[:]), ends[0][:])
+        nc.scalar.activation(out=pages[1][:].indirect(l7[:]), in_=ends[1][:], func=ACT.Copy)
+        for m in range(2):
+            nc.sync.dma_start(out[m * P : (m + 1) * P, :], pages[m][:])

@@ -42,7 +42,6 @@ def tile_list_gatedgroupboard_solo_store_postedout_kernel(
         def half(lst, h):
             return lst[:, h * (HALF // 16) : (h + 1) * (HALF // 16)]
 
-        xs_stage = sb.tile([4, 4, T // 4], I32, name="xs_stage")
         ws_stage = sb.tile([4, 4, R // 4], I32, name="ws_stage")
         xw_win = sb.tile([P, T], U32, name="xw_win")
         xs_win = sb.tile([P, T], U8, name="xs_win")
@@ -57,36 +56,40 @@ def tile_list_gatedgroupboard_solo_store_postedout_kernel(
         boards = [sb.tile([P, C], F32, name="board%d" % t) for t in range(PACK)]
         pages = [sb.tile([P, E], F32, name="page%d" % m) for m in range(2)]
 
-        nc.vector.memset(xs_win[:].bitcast(I32), 0)
+        nc.gpsimd.memset(xs_win[:].bitcast(I32), 0)
         nc.vector.memset(ws_raw[:].bitcast(I32), 0)
         nc.vector.memset(vs_win[:].bitcast(I32), 0)
-        for board in boards:
-            nc.vector.memset(board[:], 0.0)
-        for page in pages:
-            nc.vector.memset(page[:], 0.0)
+        for cleared in boards[:2] + pages:
+            nc.vector.memset(cleared[:], 0.0)
 
         def staged(scales):
             return scales[0].rearrange("(q r) c -> r q c", r=4).bitcast(I32)
 
-        nc.sync.dma_start(xs_stage[:], staged(xt_scales))
-        nc.scalar.dma_start(ws_stage[:], staged(w_scales))
+        def load_scale_rows(plane, scales):
+            for q in range(4):
+                nc.sync.dma_start(plane[32 * q : 32 * q + 4, :].bitcast(I32), scales[0, 4 * q : 4 * q + 4, :].bitcast(I32))
+
+        nc.sync.dma_start(ws_stage[:], staged(w_scales))
         nc.sync.dma_start(l1[:], offs)
-        nc.sync.dma_start(xw_win[:].bitcast(I32), xt_words[0].rearrange("p n t -> p (n t)").bitcast(I32))
         nc.sync.dma_start(ww_raw[:].bitcast(I32), w_words[0].bitcast(I32))
+        load_scale_rows(xs_win, xt_scales)
+        nc.sync.dma_start(xw_win[:].bitcast(I32), xt_words[0].rearrange("p n t -> p (n t)").bitcast(I32))
         nc.sync.dma_start(l2[:], offs2)
-        nc.sync.dma_start(l4[:], offs4)
-        nc.sync.dma_start(l3[:], offs3)
         nc.gpsimd.dma_start(sg_sb[:], sg.rearrange("(p t) o -> p (t o)", t=PACK))
         nc.gpsimd.dma_start(bg_sb[:], bg.rearrange("(p t) o -> p (t o)", t=PACK))
+        nc.sync.dma_start(l4[:], offs4)
         nc.gpsimd.dma_start(sa_sb[:], sa.rearrange("(p t) o -> p (t o)", t=PACK))
-        for m in range(2):
-            nc.gpsimd.dma_start(so_sb[m][:], so[m * P : (m + 1) * P, :])
-        nc.sync.dma_start(vw_win[:].bitcast(I32), vs_words[0].bitcast(I32))
+        nc.sync.dma_start(l3[:], offs3)
         nc.sync.dma_start(l5[:], offs5)
-        for q in range(4):
-            nc.sync.dma_start(vs_win[32 * q : 32 * q + 4, :].bitcast(I32), vs_scales[0, 4 * q : 4 * q + 4, :].bitcast(I32))
+        nc.sync.dma_start(vw_win[:].bitcast(I32), vs_words[0].bitcast(I32))
+        load_scale_rows(vs_win, vs_scales)
+        for m in range(2):
+            nc.sync.dma_start(so_sb[m][:], so[m * P : (m + 1) * P, :])
         nc.sync.dma_start(l6[:], offs6)
         nc.sync.dma_start(l7[:], offs7)
+
+        for board in boards[2:]:
+            nc.gpsimd.memset(board[:], 0.0)
 
         xw = sb.tile([P, J], U32, name="xw", align_bytes=64)
         xs = sb.tile([P, J], U8, name="xs", align_bytes=128)
@@ -97,18 +100,16 @@ def tile_list_gatedgroupboard_solo_store_postedout_kernel(
             return slice(h * HALF, (h + 1) * HALF)
 
         for q in range(4):
-            nc.vector.tensor_copy(xs_win[32 * q : 32 * q + 4, :].bitcast(I32), xs_stage[:, q, :])
-        nc.vector.tensor_copy(xs[:, cols(0)], xs_win[:].indirect(half(l1, 0)))
-        for q in range(4):
             nc.vector.tensor_copy(ws_raw[32 * q : 32 * q + 4, :].bitcast(I32), ws_stage[:, q, :])
         ws_dealt = ws_raw[:].rearrange("p (m t) -> p t m", t=PACK)
         ww_dealt = ww_raw[:].rearrange("p (m t) -> p t m", t=PACK)
         nc.vector.tensor_copy(ws[:], ws_dealt)
         for t in range(PACK):
             nc.scalar.copy(ww[:, t, :], ww_dealt[:, t, :])
+        nc.vector.tensor_copy(xs[:, cols(0)], xs_win[:].indirect(half(l1, 0)))
         nc.vector.tensor_copy(xw[:, cols(0)], xw_win[:].indirect(half(l1, 0)))
-        nc.vector.tensor_copy(xw[:, cols(1)], xw_win[:].indirect(half(l1, 1)))
         nc.vector.tensor_copy(xs[:, cols(1)], xs_win[:].indirect(half(l1, 1)))
+        nc.vector.tensor_copy(xw[:, cols(1)], xw_win[:].indirect(half(l1, 1)))
 
         a_sb = [sb.tile([P, J], F32, name="a_sb%d" % t) for t in range(PACK)]
 
@@ -120,10 +121,11 @@ def tile_list_gatedgroupboard_solo_store_postedout_kernel(
             )
             nc.scalar.copy(a_sb[t][:, js], acc[:])
 
-        first_product(0, cols(0), 0)
-        first_product(0, cols(1), 1)
-        for t in range(1, PACK):
-            first_product(t, slice(0, J), 1 + t)
+        for h in range(2):
+            for t in range(2):
+                first_product(t, cols(h), 2 * h + t)
+        for t in range(2, PACK):
+            first_product(t, slice(0, J), 2 + t)
 
         value = sb.tile([P, PACK, O], F32, name="value")
         gate = sb.tile([P, PACK, O], F32, name="gate")
@@ -137,11 +139,11 @@ def tile_list_gatedgroupboard_solo_store_postedout_kernel(
                 out=value[:, t, places], in_=boards[t][:].indirect(offs_value), func=ACT.Copy, scale=sa_sb[:, t : t + 1],
             )
 
+        for h in range(2):
+            for t in range(2):
+                nc.vector.tensor_copy(boards[t][:].indirect(half(l2, h)), a_sb[t][:, cols(h)])
         for t in range(PACK):
-            if t == 0:
-                for h in range(2):
-                    nc.vector.tensor_copy(boards[t][:].indirect(half(l2, h)), a_sb[t][:, cols(h)])
-            else:
+            if t >= 2:
                 nc.vector.tensor_copy(boards[t][:].indirect(l2[:]), a_sb[t][:])
             if t == PACK - 1:
                 for h in range(2):
@@ -154,31 +156,29 @@ def tile_list_gatedgroupboard_solo_store_postedout_kernel(
         nc.vector.tensor_copy(vw[:], vw_win[:].indirect(l5[:]))
         nc.vector.tensor_copy(vsc[:], vs_win[:].indirect(l5[:]))
 
-        hid = [sb.tile([P, HALF, PACK], BF16, name="hid%d" % h, align_bytes=64) for h in range(2)]
-        hw = [sb.tile([P, HALF], U32, name="hw%d" % h, align_bytes=64) for h in range(2)]
-        hs = [sb.tile([P, HALF], U8, name="hs%d" % h, align_bytes=64) for h in range(2)]
+        hid = sb.tile([P, O, PACK], BF16, name="hid", align_bytes=64)
+        hw = sb.tile([P, O], U32, name="hw", align_bytes=64)
+        hs = sb.tile([P, O], U8, name="hs", align_bytes=64)
         for h in range(2):
             nc.vector.tensor_tensor(
-                hid[h][:].rearrange("p (c i) t -> p c t i", i=4),
+                hid[:, cols(h), :].rearrange("p (c i) t -> p c t i", i=4),
                 value[:, :, cols(h)].rearrange("p t (c i) -> p c t i", i=4),
                 gate[:, :, cols(h)].rearrange("p t (c i) -> p c t i", i=4),
                 MULT,
             )
-        for h in range(2):
-            nc.vector.quantize_mx(out=hw[h][:].bitcast(E4M3X4), scales=hs[h][:], in_=hid[h][:].rearrange("p o t -> p (o t)"))
+        nc.vector.quantize_mx(out=hw[:].bitcast(E4M3X4), scales=hs[:], in_=hid[:].rearrange("p o t -> p (o t)"))
 
         p_sb = [sb.tile([P, O], F32, name="p_sb%d" % m) for m in range(2)]
-        for h in range(2):
-            for m in range(2):
-                acc = psum.tile([P, HALF], F32, name="acc2", tag="bank%d" % ((5 + 2 * h + m) % 8))
-                nc.tensor.matmul_mx(
-                    out=acc[:], lhsT=vw[:, cols(m)].bitcast(E2M1X4), lhsT_scale=vsc[:, cols(m)],
-                    rhs=hw[h][:].bitcast(E4M3X4), rhs_scale=hs[h][:], start=True, stop=True,
-                )
-                if m == 0:
-                    nc.scalar.copy(p_sb[m][:, cols(h)], acc[:])
-                else:
-                    nc.vector.tensor_copy(p_sb[m][:, cols(h)], acc[:])
+        for m in range(2):
+            acc = psum.tile([P, O], F32, name="acc2", tag="bank%d" % (6 + m))
+            nc.tensor.matmul_mx(
+                out=acc[:], lhsT=vw[:, cols(m)].bitcast(E2M1X4), lhsT_scale=vsc[:, cols(m)],
+                rhs=hw[:].bitcast(E4M3X4), rhs_scale=hs[:], start=True, stop=True,
+            )
+            if m == 0:
+                nc.scalar.copy(p_sb[m][:], acc[:])
+            else:
+                nc.vector.tensor_copy(p_sb[m][:], acc[:])
 
         ends = [sb.tile([P, U], F32, name="ends%d" % m) for m in range(2)]
         for m in range(2):

from contextlib import ExitStack

import concourse.mybir as mybir

K, T, J, R, C, O, N, S, U, E = 512, 1024, 256, 512, 512, 256, 256, 1024, 128, 512
FLOPS = 2 * K * R * J + 2 * R * N * O

F32 = mybir.dt.float32
BF16 = mybir.dt.bfloat16
I32 = mybir.dt.int32
U32 = mybir.dt.uint32
U16 = mybir.dt.uint16
U8 = mybir.dt.uint8
E4M3X4 = mybir.dt.float8_e4m3fn_x4
E5M2X4 = mybir.dt.float8_e5m2_x4
E2M1X4 = mybir.dt.float4_e2m1fn_x4
ACT = mybir.ActivationFunctionType
MULT = mybir.AluOpType.mult

P = 128
PACK = 4
HALF = 128


def tile_list_gatedgroupboard_solo_store_postedout_kernel(
    tc, xt_words, xt_scales, w_words, w_scales, sa, sg, bg, vs_words, vs_scales, so,
    offs, offs2, offs3, offs4, offs5, offs6, offs7, out,
):
    nc = tc.nc
    with ExitStack() as ctx:
        lists = ctx.enter_context(tc.tile_pool(name="lists", bufs=1))
        sb = ctx.enter_context(tc.tile_pool(name="sb", bufs=1))
        psum = ctx.enter_context(tc.psum_pool(name="psum", bufs=1))

        def list_tile(src, name):
            return lists.tile([P, src.shape[1]], U16, name=name)

        l1, l2, l3, l4, l5, l6, l7 = [
            list_tile(src, "list%d" % i) for i, src in enumerate((offs, offs2, offs3, offs4, offs5, offs6, offs7))
        ]

        def half(lst, h):
            return lst[:, h * (HALF // 16) : (h + 1) * (HALF // 16)]

        ws_stage = sb.tile([4, 4, R // 4], I32, name="ws_stage")
        xw_win = sb.tile([P, T], U32, name="xw_win")
        xs_win = sb.tile([P, T], U8, name="xs_win")
        ww_raw = sb.tile([P, R], U16, name="ww_raw")
        ws_raw = sb.tile([P, R], U8, name="ws_raw")
        vw_win = sb.tile([P, S], U16, name="vw_win")
        vs_win = sb.tile([P, S], U8, name="vs_win")
        sa_sb = sb.tile([P, PACK], F32, name="sa_sb")
        sg_sb = sb.tile([P, PACK], F32, name="sg_sb")
        bg_sb = sb.tile([P, PACK], F32, name="bg_sb")
        so_sb = [sb.tile([P, 1], F32, name="so_sb%d" % m) for m in range(2)]
        boards = [sb.tile([P, C], F32, name="board%d" % t) for t in range(PACK)]
        pages = [sb.tile([P, E], F32, name="page%d" % m) for m in range(2)]

        nc.gpsimd.memset(xs_win[:].bitcast(I32), 0)
        nc.vector.memset(ws_raw[:].bitcast(I32), 0)
        nc.vector.memset(vs_win[:].bitcast(I32), 0)
        for cleared in boards[:2] + pages:
            nc.vector.memset(cleared[:], 0.0)

        def staged(scales):
            return scales[0].rearrange("(q r) c -> r q c", r=4).bitcast(I32)

        def load_scale_rows(plane, scales):
            for q in range(4):
                nc.sync.dma_start(plane[32 * q : 32 * q + 4, :].bitcast(I32), scales[0, 4 * q : 4 * q + 4, :].bitcast(I32))

        nc.sync.dma_start(ws_stage[:], staged(w_scales))
        nc.sync.dma_start(l1[:], offs)
        nc.sync.dma_start(ww_raw[:].bitcast(I32), w_words[0].bitcast(I32))
        load_scale_rows(xs_win, xt_scales)
        nc.sync.dma_start(xw_win[:].bitcast(I32), xt_words[0].rearrange("p n t -> p (n t)").bitcast(I32))
        nc.sync.dma_start(l2[:], offs2)
        nc.gpsimd.dma_start(sg_sb[:], sg.rearrange("(p t) o -> p (t o)", t=PACK))
        nc.gpsimd.dma_start(bg_sb[:], bg.rearrange("(p t) o -> p (t o)", t=PACK))
        nc.sync.dma_start(l4[:], offs4)
        nc.gpsimd.dma_start(sa_sb[:], sa.rearrange("(p t) o -> p (t o)", t=PACK))
        nc.sync.dma_start(l3[:], offs3)
        nc.sync.dma_start(l5[:], offs5)
        nc.sync.dma_start(vw_win[:].bitcast(I32), vs_words[0].bitcast(I32))
        load_scale_rows(vs_win, vs_scales)
        for m in range(2):
            nc.sync.dma_start(so_sb[m][:], so[m * P : (m + 1) * P, :])
        nc.sync.dma_start(l6[:], offs6)
        nc.sync.dma_start(l7[:], offs7)

        for board in boards[2:]:
            nc.gpsimd.memset(board[:], 0.0)

        xw = sb.tile([P, J], U32, name="xw", align_bytes=64)
        xs = sb.tile([P, J], U8, name="xs", align_bytes=128)
        ww = sb.tile([P, PACK, P], U16, name="ww", align_bytes=64)
        ws = sb.tile([P, PACK, P], U8, name="ws", align_bytes=64)

        def cols(h):
            return slice(h * HALF, (h + 1) * HALF)

        for q in range(4):
            nc.vector.tensor_copy(ws_raw[32 * q : 32 * q + 4, :].bitcast(I32), ws_stage[:, q, :])
        ws_dealt = ws_raw[:].rearrange("p (m t) -> p t m", t=PACK)
        ww_dealt = ww_raw[:].rearrange("p (m t) -> p t m", t=PACK)
        nc.vector.tensor_copy(ws[:], ws_dealt)
        for t in range(PACK):
            nc.scalar.copy(ww[:, t, :], ww_dealt[:, t, :])
        nc.vector.tensor_copy(xs[:, cols(0)], xs_win[:].indirect(half(l1, 0)))
        nc.vector.tensor_copy(xw[:, cols(0)], xw_win[:].indirect(half(l1, 0)))
        nc.vector.tensor_copy(xs[:, cols(1)], xs_win[:].indirect(half(l1, 1)))
        nc.vector.tensor_copy(xw[:, cols(1)], xw_win[:].indirect(half(l1, 1)))

        a_sb = [sb.tile([P, J], F32, name="a_sb%d" % t) for t in range(PACK)]

        def first_product(t, js, bank):
            acc = psum.tile([P, js.stop - js.start], F32, name="acc", tag="bank%d" % bank)
            nc.tensor.matmul_mx(
                out=acc[:], lhsT=ww[:, t, :].bitcast(E2M1X4), lhsT_scale=ws[:, t, :],
                rhs=xw[:, js].bitcast(E5M2X4), rhs_scale=xs[:, js], start=True, stop=True,
            )
            nc.scalar.copy(a_sb[t][:, js], acc[:])

        for h in range(2):
            for t in range(2):
                first_product(t, cols(h), 2 * h + t)
        for t in range(2, PACK):
            first_product(t, slice(0, J), 2 + t)

        value = sb.tile([P, PACK, O], F32, name="value")
        gate = sb.tile([P, PACK, O], F32, name="gate")

        def look(t, places, offs_value, offs_gate):
            nc.scalar.activation(
                out=gate[:, t, places], in_=boards[t][:].indirect(offs_gate), func=ACT.Sigmoid,
                bias=bg_sb[:, t : t + 1], scale=sg_sb[:, t : t + 1],
            )
            nc.scalar.activation(
                out=value[:, t, places], in_=boards[t][:].indirect(offs_value), func=ACT.Copy, scale=sa_sb[:, t : t + 1],
            )

        for h in range(2):
            for t in range(2):
                nc.vector.tensor_copy(boards[t][:].indirect(half(l2, h)), a_sb[t][:, cols(h)])
        for t in range(PACK):
            if t >= 2:
                nc.vector.tensor_copy(boards[t][:].indirect(l2[:]), a_sb[t][:])
            if t == PACK - 1:
                for h in range(2):
                    look(t, cols(h), half(l3, h), half(l4, h))
            else:
                look(t, slice(0, O), l3[:], l4[:])

        vw = sb.tile([P, N], U16, name="vw", align_bytes=64)
        vsc = sb.tile([P, N], U8, name="vsc", align_bytes=128)
        nc.vector.tensor_copy(vw[:], vw_win[:].indirect(l5[:]))
        nc.vector.tensor_copy(vsc[:], vs_win[:].indirect(l5[:]))

        hid = sb.tile([P, O, PACK], BF16, name="hid", align_bytes=64)
        hw = sb.tile([P, O], U32, name="hw", align_bytes=64)
        hs = sb.tile([P, O], U8, name="hs", align_bytes=64)
        for h in range(2):
            nc.vector.tensor_tensor(
                hid[:, cols(h), :].rearrange("p (c i) t -> p c t i", i=4),
                value[:, :, cols(h)].rearrange("p t (c i) -> p c t i", i=4),
                gate[:, :, cols(h)].rearrange("p t (c i) -> p c t i", i=4),
                MULT,
            )
        nc.vector.quantize_mx(out=hw[:].bitcast(E4M3X4), scales=hs[:], in_=hid[:].rearrange("p o t -> p (o t)"))

        p_sb = [sb.tile([P, O], F32, name="p_sb%d" % m) for m in range(2)]
        for m in range(2):
            acc = psum.tile([P, O], F32, name="acc2", tag="bank%d" % (6 + m))
            nc.tensor.matmul_mx(
                out=acc[:], lhsT=vw[:, cols(m)].bitcast(E2M1X4), lhsT_scale=vsc[:, cols(m)],
                rhs=hw[:].bitcast(E4M3X4), rhs_scale=hs[:], start=True, stop=True,
            )
            if m == 0:
                nc.scalar.copy(p_sb[m][:], acc[:])
            else:
                nc.vector.tensor_copy(p_sb[m][:], acc[:])

        ends = [sb.tile([P, U], F32, name="ends%d" % m) for m in range(2)]
        for m in range(2):
            nc.scalar.activation(out=ends[m][:], in_=p_sb[m][:].indirect(l6[:]), func=ACT.Copy, scale=so_sb[m][:])
        nc.vector.tensor_copy(pages[0][:].indirect(l7[:]), ends[0][:])
        nc.scalar.activation(out=pages[1][:].indirect(l7[:]), in_=ends[1][:], func=ACT.Copy)
        for m in range(2):
            nc.sync.dma_start(out[m * P : (m + 1) * P, :], pages[m][:])
